import numpy as np
import ml_dtypes


def mxq(x, axis, fmt="e4m3"):
    dtype, down = {"e4m3": (ml_dtypes.float8_e4m3fn, 7), "e5m2": (ml_dtypes.float8_e5m2, 14)}[fmt]
    v = np.moveaxis(np.asarray(x, np.float32).astype(ml_dtypes.bfloat16).astype(np.float64), axis, -1)
    blocks = v.reshape(v.shape[:-1] + (-1, 32))
    amax = np.abs(blocks).max(-1, keepdims=True)
    byte = np.maximum(np.where(amax > 0, np.frexp(amax)[1] - 1 + 127, 0) - down, 1)
    scale = np.exp2(byte - 127.0)
    codes = (blocks / scale).astype(np.float32).astype(dtype).astype(np.float64)
    return np.moveaxis((codes * scale).reshape(v.shape), -1, axis)


WIDE = False


def mx_kscale(k):
    if not WIDE:
        return np.ones(k)
    levels = np.array([10, -10, 5, -5, 0])
    if k % 512:
        return np.exp2(np.random.permutation(np.resize(levels, k // 32))).repeat(32)
    a = np.empty((k // 512, 16))
    for p in range(k // 512):
        a[p, :8] = np.random.permutation(np.resize(levels, 8))
        for g in range(8):
            far = levels[np.abs(levels - a[p, g]) >= 10]
            a[p, g + 8] = far[np.random.randint(len(far))]
    return np.exp2(a.ravel()).repeat(32)


def f64(x):
    return np.asarray(x).astype(np.float64)


def striped(idx):
    return np.tile(np.asarray(idx).reshape(-1, 16).T, (8, 1)).astype(np.uint16)


def unstriped(offs):
    return offs[:16].T.reshape(-1).astype(np.int64)


K, T, I, G, U, D = 512, 2048, 1024, 256, 1024, 512


def setup_inputs():
    n = np.random.standard_normal
    idx = np.random.permutation(T)[:I]
    idx2 = np.random.permutation(U)[:G]
    fk = mx_kscale(K)
    return {
        "hid": (n((K, T)) * 2.0 / fk[:, None]).astype(np.float32),
        "wp": (n((K, D)) * 1 / np.sqrt(K) * fk[:, None]).astype(np.float32),
        "bias": (np.random.uniform(-0.5, 0.5, (D, 1))).astype(np.float32),
        "old": (n((D, U))).astype(np.float32),
        "fade": (np.random.uniform(0.5, 1.0, (1, U))).astype(np.float32),
        "offs": striped(idx),
        "offs2": striped(idx2),
    }


def reference(hid, wp, bias, old, fade, offs, offs2):
    idx = unstriped(offs)
    idx2 = unstriped(offs2)
    hs = f64(hid)[:, idx].reshape(K, G, I // G).mean(axis=2)
    wpq = mxq(f64(wp), 0, "e4m3")
    hsq = mxq(hs, 0, "e4m3")
    z = wpq.T @ hsq
    b = np.tanh(z + f64(bias))
    bf = np.zeros((D, U))
    bf[:, idx2] = b
    y = f64(old) * f64(fade) + bf
    return y

@@ -1,0 +1,125 @@
+from contextlib import ExitStack
+
+import concourse.mybir as mybir
+from concourse.masks import make_identity
+
+K, T, I, G, U, D = 512, 2048, 1024, 256, 1024, 512
+FLOPS = 2 * K * D * G
+
+F32 = mybir.dt.float32
+BF16 = mybir.dt.bfloat16
+U32 = mybir.dt.uint32
+U16 = mybir.dt.uint16
+U8 = mybir.dt.uint8
+FP8X4 = mybir.dt.float8_e4m3fn_x4
+ALU = mybir.AluOpType
+ACT = mybir.ActivationFunctionType
+AXIS_X = mybir.AxisListType.X
+
+P = 128
+PACK = 4
+PAGE = I // G
+D_TILES = D // P
+U_TILES = U // P
+BANK = 512
+HALF = I // 2
+PIECES = ((0, I // 4), (I // 4, 3 * I // 4), (3 * I // 4, I))
+
+
+def tile_attend_summaryrefresh_kernel(tc, hid, wp, bias, old, fade, offs, offs2, out):
+    nc = tc.nc
+    with ExitStack() as ctx:
+        keep = ctx.enter_context(tc.tile_pool(name="keep", bufs=1))
+        psum = ctx.enter_context(tc.psum_pool(name="psum", bufs=1))
+
+        slots = keep.tile([P, I // 16], U16, name="slots")
+        pages = keep.tile([P, G // 16], U16, name="pages")
+        planes = [keep.tile([P, T], F32, name="plane%d" % t) for t in range(PACK)]
+        w_raw = [keep.tile([P, PACK, D // 2], F32, name="w_raw%d" % h) for h in range(2)]
+        olds = [keep.tile([P, U], F32, name="old%d" % j) for j in range(D_TILES)]
+        rows = keep.tile([P, P], F32, name="rows")
+        nc.gpsimd.memset(rows[:], 0.0)
+        nc.sync.dma_start(rows[0:U_TILES, :], fade.rearrange("o (c p) -> (o c) p", p=P))
+        nc.sync.dma_start(rows[32 : 32 + D_TILES, :], bias.rearrange("(j p) o -> j (p o)", p=P))
+        hid_rows = hid.rearrange("(p t) n -> p t n", t=PACK)
+        nc.sync.dma_start(slots[:], offs)
+        for t in range(PACK):
+            nc.sync.dma_start(planes[t][:], hid_rows[:, t, :])
+        for h in range(2):
+            nc.sync.dma_start(w_raw[h][:], wp.rearrange("(p t) d -> p t d", t=PACK)[:, :, h * (D // 2) : (h + 1) * (D // 2)])
+        nc.sync.dma_start(pages[:], offs2)
+        for j in range(D_TILES):
+            nc.sync.dma_start(olds[j][:], old[j * P : (j + 1) * P, :])
+
+        ident = keep.tile([P, P], F32, name="ident")
+        make_identity(nc, ident[:])
+        turned = psum.tile([P, P], F32, name="turned")
+        nc.tensor.transpose(turned[:], rows[:], ident[:])
+        cols = keep.tile([P, 64], F32, name="cols")
+        nc.scalar.copy(cols[:], turned[:, 0:64])
+        spreads = []
+        for h in range(U // BANK):
+            spread = psum.tile([P, BANK], F32, name="spread%d" % h)
+            for c in range(BANK // P):
+                col = h * (BANK // P) + c
+                nc.tensor.transpose(spread[:, c * P : (c + 1) * P], cols[:, col : col + 1].to_broadcast([P, P]), ident[:])
+            spreads.append(spread)
+
+        placed = [keep.tile([P, U], F32, name="placed%d" % j) for j in range(D_TILES)]
+        for j in range(D_TILES):
+            nc.vector.memset(placed[j][:].bitcast(U32), 0)
+
+        h_in = keep.tile([P, G, PACK], BF16, name="h_in", align_bytes=64)
+        for t in range(PACK):
+            got = keep.tile([P, I], F32, name="got%d" % t)
+            for lo, hi in PIECES:
+                window = planes[t][:].indirect(slots[:, lo // 16 : hi // 16])
+                if hi - lo == HALF:
+                    nc.vector.tensor_scalar(got[:, lo:hi], window, 1.0 / PAGE, 0.0, ALU.mult, ALU.add)
+                else:
+                    nc.scalar.activation(got[:, lo:hi], window, ACT.Copy, scale=1.0 / PAGE)
+            for lo, hi in PIECES:
+                with nc.allow_low_precision(reason="sums in float32, rounds once"):
+                    nc.vector.tensor_reduce(h_in[:, lo // PAGE : hi // PAGE, t], got[:, lo:hi].rearrange("p (g i) -> p g i", i=PAGE), AXIS_X, ALU.add)
+        h_codes = keep.tile([P, G], U32, name="h_codes", align_bytes=64)
+        h_scales = keep.tile([P, G], U8, name="h_scales", align_bytes=64)
+        for s in range(2):
+            cs = slice(s * (G // 2), (s + 1) * (G // 2))
+            nc.vector.quantize_mx(out=h_codes[:, cs].bitcast(FP8X4), scales=h_scales[:, cs], in_=h_in[:, cs, :].rearrange("p g t -> p (g t)"))
+
+        zs = []
+        for j in range(D_TILES):
+            w_in = keep.tile([P, P, PACK], BF16, name="w_in%d" % j, align_bytes=64)
+            src = w_raw[j // 2][:, :, (j % 2) * P : (j % 2 + 1) * P].rearrange("p t (c i) -> p c t i", i=4)
+            dst = w_in[:].rearrange("p (c i) t -> p c t i", i=4)
+            nc.scalar.copy(dst, src)
+            w_codes = keep.tile([P, P], U32, name="w_codes%d" % j, align_bytes=64)
+            w_scales = keep.tile([P, P], U8, name="w_scales%d" % j, align_bytes=64)
+            nc.vector.quantize_mx(out=w_codes[:].bitcast(FP8X4), scales=w_scales[:], in_=w_in[:].rearrange("p m t -> p (m t)"))
+            z = psum.tile([P, G], F32, name="z%d" % j)
+            nc.tensor.matmul_mx(out=z[:], lhsT=w_codes[:].bitcast(FP8X4), lhsT_scale=w_scales[:],
+                                rhs=h_codes[:].bitcast(FP8X4), rhs_scale=h_scales[:], start=True, stop=True)
+            zs.append(z)
+
+        fresh = [keep.tile([P, G], F32, name="fresh%d" % j) for j in range(D_TILES)]
+        faded = [keep.tile([P, U], F32, name="faded%d" % j) for j in range(D_TILES)]
+
+        def squash(j):
+            nc.scalar.activation(fresh[j][:], zs[j][:], ACT.Tanh, bias=cols[:, 32 + j : 33 + j])
+
+        squash(0)
+        for j in range(D_TILES):
+            if j + 1 < D_TILES:
+                squash(j + 1)
+            nc.scalar.activation(placed[j][:].indirect(pages[:]), fresh[j][:], ACT.Copy)
+        for j in range(D_TILES):
+            for h in range(U // BANK):
+                hs = slice(h * BANK, (h + 1) * BANK)
+                nc.vector.tensor_tensor(faded[j][:, hs], olds[j][:, hs], spreads[h][:], ALU.mult)
+        for j in range(D_TILES):
+            total = olds[(j + 2) % D_TILES]
+            cuts = 2 if j == D_TILES - 1 else 1
+            for c in range(cuts):
+                us = slice(c * (U // cuts), (c + 1) * (U // cuts))
+                nc.vector.tensor_tensor(total[:, us], faded[j][:, us], placed[j][:, us], ALU.add)
+                nc.sync.dma_start(out[j * P : (j + 1) * P, us], total[:, us])

@@ -22,28 +22,32 @@ PAGE = I // G
 D_TILES = D // P
 U_TILES = U // P
 BANK = 512
-HALF = I // 2
-PIECES = ((0, I // 4), (I // 4, 3 * I // 4), (3 * I // 4, I))
+BIAS_ROW = 32
+V_SHARE = 256
+HEAD = 640
 
 
 def tile_attend_summaryrefresh_kernel(tc, hid, wp, bias, old, fade, offs, offs2, out):
     nc = tc.nc
     with ExitStack() as ctx:
         keep = ctx.enter_context(tc.tile_pool(name="keep", bufs=1))
+        reuse = ctx.enter_context(tc.tile_pool(name="reuse", bufs=1))
         psum = ctx.enter_context(tc.psum_pool(name="psum", bufs=1))
 
         slots = keep.tile([P, I // 16], U16, name="slots")
         pages = keep.tile([P, G // 16], U16, name="pages")
-        planes = [keep.tile([P, T], F32, name="plane%d" % t) for t in range(PACK)]
+        planes = [keep.tile([P, T], F32, name="plane%d" % t) for t in range(PACK - 1)]
+        planes.append(reuse.tile([P, T], F32, name="plane_last", offset=0, align_bytes=64))
         w_raw = [keep.tile([P, PACK, D // 2], F32, name="w_raw%d" % h) for h in range(2)]
         olds = [keep.tile([P, U], F32, name="old%d" % j) for j in range(D_TILES)]
         rows = keep.tile([P, P], F32, name="rows")
         nc.gpsimd.memset(rows[:], 0.0)
-        nc.sync.dma_start(rows[0:U_TILES, :], fade.rearrange("o (c p) -> (o c) p", p=P))
-        nc.sync.dma_start(rows[32 : 32 + D_TILES, :], bias.rearrange("(j p) o -> j (p o)", p=P))
         hid_rows = hid.rearrange("(p t) n -> p t n", t=PACK)
+        nc.sync.dma_start(planes[0][:], hid_rows[:, 0, :])
         nc.sync.dma_start(slots[:], offs)
-        for t in range(PACK):
+        nc.sync.dma_start(rows[0:U_TILES, :], fade.rearrange("o (c p) -> (o c) p", p=P))
+        nc.sync.dma_start(rows[BIAS_ROW : BIAS_ROW + D_TILES, :], bias.rearrange("(j p) o -> j (p o)", p=P))
+        for t in range(1, PACK):
             nc.sync.dma_start(planes[t][:], hid_rows[:, t, :])
         for h in range(2):
             nc.sync.dma_start(w_raw[h][:], wp.rearrange("(p t) d -> p t d", t=PACK)[:, :, h * (D // 2) : (h + 1) * (D // 2)])
@@ -55,8 +59,8 @@ def tile_attend_summaryrefresh_kernel(tc, hid, wp, bias, old, fade, offs, offs2,
         make_identity(nc, ident[:])
         turned = psum.tile([P, P], F32, name="turned")
         nc.tensor.transpose(turned[:], rows[:], ident[:])
-        cols = keep.tile([P, 64], F32, name="cols")
-        nc.scalar.copy(cols[:], turned[:, 0:64])
+        cols = keep.tile([P, 2 * BIAS_ROW], F32, name="cols")
+        nc.vector.tensor_copy(cols[:], turned[:, 0 : 2 * BIAS_ROW])
         spreads = []
         for h in range(U // BANK):
             spread = psum.tile([P, BANK], F32, name="spread%d" % h)
@@ -67,57 +71,79 @@ def tile_attend_summaryrefresh_kernel(tc, hid, wp, bias, old, fade, offs, offs2,
 
         placed = [keep.tile([P, U], F32, name="placed%d" % j) for j in range(D_TILES)]
         for j in range(D_TILES):
-            nc.vector.memset(placed[j][:].bitcast(U32), 0)
+            nc.vector.memset(placed[j][:], 0.0)
 
-        h_in = keep.tile([P, G, PACK], BF16, name="h_in", align_bytes=64)
+        sums = keep.tile([P, PACK, G], F32, name="sums")
         for t in range(PACK):
-            got = keep.tile([P, I], F32, name="got%d" % t)
-            for lo, hi in PIECES:
-                window = planes[t][:].indirect(slots[:, lo // 16 : hi // 16])
-                if hi - lo == HALF:
-                    nc.vector.tensor_scalar(got[:, lo:hi], window, 1.0 / PAGE, 0.0, ALU.mult, ALU.add)
-                else:
-                    nc.scalar.activation(got[:, lo:hi], window, ACT.Copy, scale=1.0 / PAGE)
-            for lo, hi in PIECES:
-                with nc.allow_low_precision(reason="sums in float32, rounds once"):
-                    nc.vector.tensor_reduce(h_in[:, lo // PAGE : hi // PAGE, t], got[:, lo:hi].rearrange("p (g i) -> p g i", i=PAGE), AXIS_X, ALU.add)
+            head = keep.tile([P, HEAD], F32, name="head%d" % t)
+            tail = keep.tile([P, I - HEAD], F32, name="tail%d" % t)
+
+            def listed(lo, hi):
+                return planes[t][:].indirect(slots[:, lo // 16 : hi // 16])
+
+            nc.vector.tensor_copy(head[:, 0:V_SHARE], listed(0, V_SHARE))
+            nc.scalar.activation(head[:, V_SHARE:HEAD], listed(V_SHARE, HEAD), ACT.Copy)
+            nc.scalar.activation(tail[:], listed(HEAD, I), ACT.Copy)
+            for piece, lo, hi in ((head, 0, HEAD), (tail, HEAD, I)):
+                nc.vector.tensor_reduce(sums[:, t, lo // PAGE : hi // PAGE], piece[:].rearrange("p (g i) -> p g i", i=PAGE), AXIS_X, ALU.add)
+
+        w_in = [reuse.tile([P, P, PACK], BF16, name="w_in%d" % j, offset=j * 1024, align_bytes=64) for j in range(D_TILES)]
+
+        def weave_w(j):
+            src = w_raw[j // 2][:, :, (j % 2) * P : (j % 2 + 1) * P].rearrange("p t (c i) -> p c t i", i=4)
+            nc.scalar.copy(w_in[j][:].rearrange("p (c i) t -> p c t i", i=4), src)
+
+        h_in = [reuse.tile([P, G // 2, PACK], BF16, name="h_in%d" % s, offset=8192 + s * 1024, align_bytes=64) for s in range(2)]
         h_codes = keep.tile([P, G], U32, name="h_codes", align_bytes=64)
         h_scales = keep.tile([P, G], U8, name="h_scales", align_bytes=64)
+        halves = [slice(s * (G // 2), (s + 1) * (G // 2)) for s in range(2)]
+        weave_w(0)
         for s in range(2):
-            cs = slice(s * (G // 2), (s + 1) * (G // 2))
-            nc.vector.quantize_mx(out=h_codes[:, cs].bitcast(FP8X4), scales=h_scales[:, cs], in_=h_in[:, cs, :].rearrange("p g t -> p (g t)"))
+            src = sums[:, :, halves[s]].rearrange("p t (c i) -> p c t i", i=4)
+            dst = h_in[s][:].rearrange("p (c i) t -> p c t i", i=4)
+            if s == 0 or True:
+                nc.vector.tensor_scalar(dst, src, 1.0 / PAGE, None, ALU.mult)
+            else:
+                nc.scalar.activation(dst, src, ACT.Copy, scale=1.0 / PAGE)
+        for s in range(2):
+            nc.vector.quantize_mx(out=h_codes[:, halves[s]].bitcast(FP8X4), scales=h_scales[:, halves[s]], in_=h_in[s][:].rearrange("p g t -> p (g t)"))
 
         zs = []
         for j in range(D_TILES):
-            w_in = keep.tile([P, P, PACK], BF16, name="w_in%d" % j, align_bytes=64)
-            src = w_raw[j // 2][:, :, (j % 2) * P : (j % 2 + 1) * P].rearrange("p t (c i) -> p c t i", i=4)
-            dst = w_in[:].rearrange("p (c i) t -> p c t i", i=4)
-            nc.scalar.copy(dst, src)
+            if j > 0:
+                weave_w(j)
             w_codes = keep.tile([P, P], U32, name="w_codes%d" % j, align_bytes=64)
             w_scales = keep.tile([P, P], U8, name="w_scales%d" % j, align_bytes=64)
-            nc.vector.quantize_mx(out=w_codes[:].bitcast(FP8X4), scales=w_scales[:], in_=w_in[:].rearrange("p m t -> p (m t)"))
+            nc.vector.quantize_mx(out=w_codes[:].bitcast(FP8X4), scales=w_scales[:], in_=w_in[j][:].rearrange("p m t -> p (m t)"))
             z = psum.tile([P, G], F32, name="z%d" % j)
             nc.tensor.matmul_mx(out=z[:], lhsT=w_codes[:].bitcast(FP8X4), lhsT_scale=w_scales[:],
                                 rhs=h_codes[:].bitcast(FP8X4), rhs_scale=h_scales[:], start=True, stop=True)
             zs.append(z)
 
         fresh = [keep.tile([P, G], F32, name="fresh%d" % j) for j in range(D_TILES)]
-        faded = [keep.tile([P, U], F32, name="faded%d" % j) for j in range(D_TILES)]
+        faded = [reuse.tile([P, U], F32, name="faded%d" % j, offset=(8192, 0, 12288, 16384)[j], align_bytes=64) for j in range(D_TILES)]
 
         def squash(j):
-            nc.scalar.activation(fresh[j][:], zs[j][:], ACT.Tanh, bias=cols[:, 32 + j : 33 + j])
+            nc.scalar.activation(fresh[j][:], zs[j][:], ACT.Tanh, bias=cols[:, BIAS_ROW + j : BIAS_ROW + j + 1])
 
         squash(0)
         for j in range(D_TILES):
             if j + 1 < D_TILES:
                 squash(j + 1)
             nc.scalar.activation(placed[j][:].indirect(pages[:]), fresh[j][:], ACT.Copy)
-        for j in range(D_TILES):
+
+        def fade_old(j):
             for h in range(U // BANK):
                 hs = slice(h * BANK, (h + 1) * BANK)
                 nc.vector.tensor_tensor(faded[j][:, hs], olds[j][:, hs], spreads[h][:], ALU.mult)
+
+        AHEAD = 2
+        for j in range(AHEAD):
+            fade_old(j)
         for j in range(D_TILES):
-            total = olds[(j + 2) % D_TILES]
+            if j + AHEAD < D_TILES:
+                fade_old(j + AHEAD)
+            total = olds[(j + AHEAD) % D_TILES]
             cuts = 2 if j == D_TILES - 1 else 1
             for c in range(cuts):
                 us = slice(c * (U // cuts), (c + 1) * (U // cuts))

@@ -40,6 +40,10 @@ def tile_attend_summaryrefresh_kernel(tc, hid, wp, bias, old, fade, offs, offs2,
         planes.append(reuse.tile([P, T], F32, name="plane_last", offset=0, align_bytes=64))
         w_raw = [keep.tile([P, PACK, D // 2], F32, name="w_raw%d" % h) for h in range(2)]
         olds = [keep.tile([P, U], F32, name="old%d" % j) for j in range(D_TILES)]
+        seed = keep.tile([P, 1], F32, name="seed")
+        nc.vector.memset(seed[:], 0.0)
+        warm = keep.tile([P, 1], F32, name="warm")
+        nc.scalar.activation(warm[:], seed[:], ACT.Tanh)
         rows = keep.tile([P, P], F32, name="rows")
         nc.gpsimd.memset(rows[:], 0.0)
         hid_rows = hid.rearrange("(p t) n -> p t n", t=PACK)

@@ -19,12 +19,26 @@ AXIS_X = mybir.AxisListType.X
 P = 128
 PACK = 4
 PAGE = I // G
+STRIPE = 16
 D_TILES = D // P
-U_TILES = U // P
 BANK = 512
+RUN = 4
 BIAS_ROW = 32
-V_SHARE = 256
+
 HEAD = 640
+VECTOR_SHARE = (256, 256, 256, 384)
+
+TILE_BYTES = 4 * U
+LAST_PLANE_AT = 0
+W_IN_AT = (0, TILE_BYTES - 1024)
+H_IN_AT = (2 * TILE_BYTES, 2 * TILE_BYTES + 1024)
+FADED_AT = (2 * TILE_BYTES, 0, TILE_BYTES)
+SUMS_AT = 3 * TILE_BYTES
+W_CODES_AT = (SUMS_AT, 4 * TILE_BYTES)
+
+
+def halves(n):
+    return [slice(0, n // 2), slice(n // 2, n)]
 
 
 def tile_attend_summaryrefresh_kernel(tc, hid, wp, bias, old, fade, offs, offs2, out):
@@ -34,27 +48,28 @@ def tile_attend_summaryrefresh_kernel(tc, hid, wp, bias, old, fade, offs, offs2,
         reuse = ctx.enter_context(tc.tile_pool(name="reuse", bufs=1))
         psum = ctx.enter_context(tc.psum_pool(name="psum", bufs=1))
 
-        slots = keep.tile([P, I // 16], U16, name="slots")
-        pages = keep.tile([P, G // 16], U16, name="pages")
-        planes = [keep.tile([P, T], F32, name="plane%d" % t) for t in range(PACK - 1)]
-        planes.append(reuse.tile([P, T], F32, name="plane_last", offset=0, align_bytes=64))
-        w_raw = [keep.tile([P, PACK, D // 2], F32, name="w_raw%d" % h) for h in range(2)]
-        olds = [keep.tile([P, U], F32, name="old%d" % j) for j in range(D_TILES)]
         seed = keep.tile([P, 1], F32, name="seed")
         nc.vector.memset(seed[:], 0.0)
         warm = keep.tile([P, 1], F32, name="warm")
         nc.scalar.activation(warm[:], seed[:], ACT.Tanh)
+
+        slots = keep.tile([P, I // STRIPE], U16, name="slots")
+        pages = keep.tile([P, G // STRIPE], U16, name="pages")
+        planes = [keep.tile([P, T], F32, name="plane%d" % t) for t in range(PACK - 1)]
+        planes.append(reuse.tile([P, T], F32, name="plane_last", offset=LAST_PLANE_AT, align_bytes=64))
+        w_raw = [keep.tile([P, PACK, D // 2], F32, name="w_raw%d" % h) for h in range(2)]
+        olds = [keep.tile([P, U], F32, name="old%d" % j) for j in range(D_TILES)]
         rows = keep.tile([P, P], F32, name="rows")
         nc.gpsimd.memset(rows[:], 0.0)
-        hid_rows = hid.rearrange("(p t) n -> p t n", t=PACK)
-        nc.sync.dma_start(planes[0][:], hid_rows[:, 0, :])
+        hid_planes = hid.rearrange("(p t) n -> p t n", t=PACK)
+        nc.sync.dma_start(planes[0][:], hid_planes[:, 0, :])
         nc.sync.dma_start(slots[:], offs)
-        nc.sync.dma_start(rows[0:U_TILES, :], fade.rearrange("o (c p) -> (o c) p", p=P))
+        nc.sync.dma_start(rows[0 : U // P, :], fade.rearrange("o (c p) -> (o c) p", p=P))
         nc.sync.dma_start(rows[BIAS_ROW : BIAS_ROW + D_TILES, :], bias.rearrange("(j p) o -> j (p o)", p=P))
         for t in range(1, PACK):
-            nc.sync.dma_start(planes[t][:], hid_rows[:, t, :])
-        for h in range(2):
-            nc.sync.dma_start(w_raw[h][:], wp.rearrange("(p t) d -> p t d", t=PACK)[:, :, h * (D // 2) : (h + 1) * (D // 2)])
+            nc.sync.dma_start(planes[t][:], hid_planes[:, t, :])
+        for h, ds in enumerate(halves(D)):
+            nc.sync.dma_start(w_raw[h][:], wp.rearrange("(p t) d -> p t d", t=PACK)[:, :, ds])
         nc.sync.dma_start(pages[:], offs2)
         for j in range(D_TILES):
             nc.sync.dma_start(olds[j][:], old[j * P : (j + 1) * P, :])
@@ -65,70 +80,75 @@ def tile_attend_summaryrefresh_kernel(tc, hid, wp, bias, old, fade, offs, offs2,
         nc.tensor.transpose(turned[:], rows[:], ident[:])
         cols = keep.tile([P, 2 * BIAS_ROW], F32, name="cols")
         nc.vector.tensor_copy(cols[:], turned[:, 0 : 2 * BIAS_ROW])
-        spreads = []
-        for h in range(U // BANK):
-            spread = psum.tile([P, BANK], F32, name="spread%d" % h)
-            for c in range(BANK // P):
-                col = h * (BANK // P) + c
-                nc.tensor.transpose(spread[:, c * P : (c + 1) * P], cols[:, col : col + 1].to_broadcast([P, P]), ident[:])
-            spreads.append(spread)
+        fade_banks = [psum.tile([P, BANK], F32, name="fade_bank%d" % h) for h in range(U // BANK)]
+        for c in range(U // P):
+            h, x = divmod(c * P, BANK)
+            nc.tensor.transpose(fade_banks[h][:, x : x + P], cols[:, c : c + 1].to_broadcast([P, P]), ident[:])
 
         placed = [keep.tile([P, U], F32, name="placed%d" % j) for j in range(D_TILES)]
         for j in range(D_TILES):
             nc.vector.memset(placed[j][:], 0.0)
 
-        sums = keep.tile([P, PACK, G], F32, name="sums")
+        sums = reuse.tile([P, PACK, G], F32, name="sums", offset=SUMS_AT, align_bytes=64)
         for t in range(PACK):
             head = keep.tile([P, HEAD], F32, name="head%d" % t)
             tail = keep.tile([P, I - HEAD], F32, name="tail%d" % t)
-
-            def listed(lo, hi):
-                return planes[t][:].indirect(slots[:, lo // 16 : hi // 16])
-
-            nc.vector.tensor_copy(head[:, 0:V_SHARE], listed(0, V_SHARE))
-            nc.scalar.activation(head[:, V_SHARE:HEAD], listed(V_SHARE, HEAD), ACT.Copy)
-            nc.scalar.activation(tail[:], listed(HEAD, I), ACT.Copy)
+            share = VECTOR_SHARE[t]
+            nc.vector.tensor_copy(head[:, 0:share], planes[t][:].indirect(slots[:, 0 : share // STRIPE]))
+            nc.scalar.activation(
+                head[:, share:HEAD], planes[t][:].indirect(slots[:, share // STRIPE : HEAD // STRIPE]), ACT.Copy
+            )
+            nc.scalar.activation(tail[:], planes[t][:].indirect(slots[:, HEAD // STRIPE : I // STRIPE]), ACT.Copy)
             for piece, lo, hi in ((head, 0, HEAD), (tail, HEAD, I)):
-                nc.vector.tensor_reduce(sums[:, t, lo // PAGE : hi // PAGE], piece[:].rearrange("p (g i) -> p g i", i=PAGE), AXIS_X, ALU.add)
+                nc.vector.tensor_reduce(
+                    sums[:, t, lo // PAGE : hi // PAGE], piece[:].rearrange("p (g i) -> p g i", i=PAGE), AXIS_X, ALU.add
+                )
 
-        w_in = [reuse.tile([P, P, PACK], BF16, name="w_in%d" % j, offset=j * 1024, align_bytes=64) for j in range(D_TILES)]
+        def woven(src, dst):
+            return src.rearrange("p t (c i) -> p c t i", i=RUN), dst.rearrange("p (c i) t -> p c t i", i=RUN)
 
-        def weave_w(j):
-            src = w_raw[j // 2][:, :, (j % 2) * P : (j % 2 + 1) * P].rearrange("p t (c i) -> p c t i", i=4)
-            nc.scalar.copy(w_in[j][:].rearrange("p (c i) t -> p c t i", i=4), src)
+        def quantise(codes, scales, values):
+            nc.vector.quantize_mx(out=codes.bitcast(FP8X4), scales=scales, in_=values.rearrange("p c t -> p (c t)"))
 
-        h_in = [reuse.tile([P, G // 2, PACK], BF16, name="h_in%d" % s, offset=8192 + s * 1024, align_bytes=64) for s in range(2)]
+        w_in = []
+        for h in range(2):
+            w_in.append(reuse.tile([P, D // 2, PACK], BF16, name="w_in%d" % h, offset=W_IN_AT[h], align_bytes=64))
+            src, dst = woven(w_raw[h][:], w_in[h][:])
+            nc.scalar.copy(dst, src)
+
+        h_in = []
+        for s, gs in enumerate(halves(G)):
+            h_in.append(reuse.tile([P, G // 2, PACK], BF16, name="h_in%d" % s, offset=H_IN_AT[s], align_bytes=64))
+            src, dst = woven(sums[:, :, gs], h_in[s][:])
+            nc.vector.tensor_scalar(dst, src, 1.0 / PAGE, None, ALU.mult)
+
+        w_codes = [
+            reuse.tile([P, D // 2], U32, name="w_codes%d" % h, offset=W_CODES_AT[h], align_bytes=64) for h in range(2)
+        ]
+        w_scales = [keep.tile([P, D // 2], U8, name="w_scales%d" % h, align_bytes=64) for h in range(2)]
         h_codes = keep.tile([P, G], U32, name="h_codes", align_bytes=64)
         h_scales = keep.tile([P, G], U8, name="h_scales", align_bytes=64)
-        halves = [slice(s * (G // 2), (s + 1) * (G // 2)) for s in range(2)]
-        weave_w(0)
-        for s in range(2):
-            src = sums[:, :, halves[s]].rearrange("p t (c i) -> p c t i", i=4)
-            dst = h_in[s][:].rearrange("p (c i) t -> p c t i", i=4)
-            if s == 0 or True:
-                nc.vector.tensor_scalar(dst, src, 1.0 / PAGE, None, ALU.mult)
-            else:
-                nc.scalar.activation(dst, src, ACT.Copy, scale=1.0 / PAGE)
-        for s in range(2):
-            nc.vector.quantize_mx(out=h_codes[:, halves[s]].bitcast(FP8X4), scales=h_scales[:, halves[s]], in_=h_in[s][:].rearrange("p g t -> p (g t)"))
+        for s, gs in enumerate(halves(G)):
+            quantise(h_codes[:, gs], h_scales[:, gs], h_in[s][:])
+            quantise(w_codes[s][:], w_scales[s][:], w_in[s][:])
 
-        zs = []
+        z = [psum.tile([P, G], F32, name="z%d" % j) for j in range(D_TILES)]
         for j in range(D_TILES):
-            if j > 0:
-                weave_w(j)
-            w_codes = keep.tile([P, P], U32, name="w_codes%d" % j, align_bytes=64)
-            w_scales = keep.tile([P, P], U8, name="w_scales%d" % j, align_bytes=64)
-            nc.vector.quantize_mx(out=w_codes[:].bitcast(FP8X4), scales=w_scales[:], in_=w_in[j][:].rearrange("p m t -> p (m t)"))
-            z = psum.tile([P, G], F32, name="z%d" % j)
-            nc.tensor.matmul_mx(out=z[:], lhsT=w_codes[:].bitcast(FP8X4), lhsT_scale=w_scales[:],
-                                rhs=h_codes[:].bitcast(FP8X4), rhs_scale=h_scales[:], start=True, stop=True)
-            zs.append(z)
+            h, m = divmod(j * P, D // 2)
+            nc.tensor.matmul_mx(
+                out=z[j][:],
+                lhsT=w_codes[h][:, m : m + P].bitcast(FP8X4),
+                lhsT_scale=w_scales[h][:, m : m + P],
+                rhs=h_codes[:].bitcast(FP8X4),
+                rhs_scale=h_scales[:],
+                start=True,
+                stop=True,
+            )
 
         fresh = [keep.tile([P, G], F32, name="fresh%d" % j) for j in range(D_TILES)]
-        faded = [reuse.tile([P, U], F32, name="faded%d" % j, offset=(8192, 0, 12288, 16384)[j], align_bytes=64) for j in range(D_TILES)]
 
         def squash(j):
-            nc.scalar.activation(fresh[j][:], zs[j][:], ACT.Tanh, bias=cols[:, BIAS_ROW + j : BIAS_ROW + j + 1])
+            nc.scalar.activation(fresh[j][:], z[j][:], ACT.Tanh, bias=cols[:, BIAS_ROW + j : BIAS_ROW + j + 1])
 
         squash(0)
         for j in range(D_TILES):
@@ -136,20 +156,27 @@ def tile_attend_summaryrefresh_kernel(tc, hid, wp, bias, old, fade, offs, offs2,
                 squash(j + 1)
             nc.scalar.activation(placed[j][:].indirect(pages[:]), fresh[j][:], ACT.Copy)
 
-        def fade_old(j):
-            for h in range(U // BANK):
-                hs = slice(h * BANK, (h + 1) * BANK)
-                nc.vector.tensor_tensor(faded[j][:, hs], olds[j][:, hs], spreads[h][:], ALU.mult)
+        last = D_TILES - 1
+        faded = [reuse.tile([P, U], F32, name="faded%d" % j, offset=FADED_AT[j], align_bytes=64) for j in range(last)]
+        faded.append(faded[0])
+        totals = [olds[1], olds[0]] + olds[2:]
+        banks = halves(U)
 
-        AHEAD = 2
-        for j in range(AHEAD):
-            fade_old(j)
-        for j in range(D_TILES):
-            if j + AHEAD < D_TILES:
-                fade_old(j + AHEAD)
-            total = olds[(j + AHEAD) % D_TILES]
-            cuts = 2 if j == D_TILES - 1 else 1
-            for c in range(cuts):
-                us = slice(c * (U // cuts), (c + 1) * (U // cuts))
-                nc.vector.tensor_tensor(total[:, us], faded[j][:, us], placed[j][:, us], ALU.add)
-                nc.sync.dma_start(out[j * P : (j + 1) * P, us], total[:, us])
+        def fade_old(j, h):
+            nc.vector.tensor_tensor(faded[j][:, banks[h]], olds[j][:, banks[h]], fade_banks[h][:], ALU.mult)
+
+        def finish(j, us):
+            nc.vector.tensor_tensor(totals[j][:, us], faded[j][:, us], placed[j][:, us], ALU.add)
+            nc.sync.dma_start(out[j * P : (j + 1) * P, us], totals[j][:, us])
+
+        whole = slice(0, U)
+        for j in range(last):
+            for h in range(len(banks)):
+                fade_old(j, h)
+        for j in range(last - 1):
+            finish(j, whole)
+        fade_old(last, 0)
+        finish(last - 1, whole)
+        fade_old(last, 1)
+        for us in banks:
+            finish(last, us)

@@ -26,7 +26,7 @@ RUN = 4
 BIAS_ROW = 32
 
 HEAD = 640
-VECTOR_SHARE = (256, 256, 256, 384)
+VECTOR_SHARE = 256
 
 TILE_BYTES = 4 * U
 LAST_PLANE_AT = 0
@@ -93,10 +93,9 @@ def tile_attend_summaryrefresh_kernel(tc, hid, wp, bias, old, fade, offs, offs2,
         for t in range(PACK):
             head = keep.tile([P, HEAD], F32, name="head%d" % t)
             tail = keep.tile([P, I - HEAD], F32, name="tail%d" % t)
-            share = VECTOR_SHARE[t]
-            nc.vector.tensor_copy(head[:, 0:share], planes[t][:].indirect(slots[:, 0 : share // STRIPE]))
+            nc.vector.tensor_copy(head[:, 0:VECTOR_SHARE], planes[t][:].indirect(slots[:, 0 : VECTOR_SHARE // STRIPE]))
             nc.scalar.activation(
-                head[:, share:HEAD], planes[t][:].indirect(slots[:, share // STRIPE : HEAD // STRIPE]), ACT.Copy
+                head[:, VECTOR_SHARE:HEAD], planes[t][:].indirect(slots[:, VECTOR_SHARE // STRIPE : HEAD // STRIPE]), ACT.Copy
             )
             nc.scalar.activation(tail[:], planes[t][:].indirect(slots[:, HEAD // STRIPE : I // STRIPE]), ACT.Copy)
             for piece, lo, hi in ((head, 0, HEAD), (tail, HEAD, I)):

from contextlib import ExitStack

import concourse.mybir as mybir
from concourse.masks import make_identity

K, T, I, G, U, D = 512, 2048, 1024, 256, 1024, 512
FLOPS = 2 * K * D * G

F32 = mybir.dt.float32
BF16 = mybir.dt.bfloat16
U32 = mybir.dt.uint32
U16 = mybir.dt.uint16
U8 = mybir.dt.uint8
FP8X4 = mybir.dt.float8_e4m3fn_x4
ALU = mybir.AluOpType
ACT = mybir.ActivationFunctionType
AXIS_X = mybir.AxisListType.X

P = 128
PACK = 4
PAGE = I // G
STRIPE = 16
D_TILES = D // P
BANK = 512
RUN = 4
BIAS_ROW = 32

HEAD = 640
VECTOR_SHARE = 256

TILE_BYTES = 4 * U
LAST_PLANE_AT = 0
W_IN_AT = (0, TILE_BYTES - 1024)
H_IN_AT = (2 * TILE_BYTES, 2 * TILE_BYTES + 1024)
FADED_AT = (2 * TILE_BYTES, 0, TILE_BYTES)
SUMS_AT = 3 * TILE_BYTES
W_CODES_AT = (SUMS_AT, 4 * TILE_BYTES)


def halves(n):
    return [slice(0, n // 2), slice(n // 2, n)]


def tile_attend_summaryrefresh_kernel(tc, hid, wp, bias, old, fade, offs, offs2, out):
    nc = tc.nc
    with ExitStack() as ctx:
        keep = ctx.enter_context(tc.tile_pool(name="keep", bufs=1))
        reuse = ctx.enter_context(tc.tile_pool(name="reuse", bufs=1))
        psum = ctx.enter_context(tc.psum_pool(name="psum", bufs=1))

        seed = keep.tile([P, 1], F32, name="seed")
        nc.vector.memset(seed[:], 0.0)
        warm = keep.tile([P, 1], F32, name="warm")
        nc.scalar.activation(warm[:], seed[:], ACT.Tanh)

        slots = keep.tile([P, I // STRIPE], U16, name="slots")
        pages = keep.tile([P, G // STRIPE], U16, name="pages")
        planes = [keep.tile([P, T], F32, name="plane%d" % t) for t in range(PACK - 1)]
        planes.append(reuse.tile([P, T], F32, name="plane_last", offset=LAST_PLANE_AT, align_bytes=64))
        w_raw = [keep.tile([P, PACK, D // 2], F32, name="w_raw%d" % h) for h in range(2)]
        olds = [keep.tile([P, U], F32, name="old%d" % j) for j in range(D_TILES)]
        rows = keep.tile([P, P], F32, name="rows")
        nc.gpsimd.memset(rows[:], 0.0)
        hid_planes = hid.rearrange("(p t) n -> p t n", t=PACK)
        nc.sync.dma_start(planes[0][:], hid_planes[:, 0, :])
        nc.sync.dma_start(slots[:], offs)
        nc.sync.dma_start(rows[0 : U // P, :], fade.rearrange("o (c p) -> (o c) p", p=P))
        nc.sync.dma_start(rows[BIAS_ROW : BIAS_ROW + D_TILES, :], bias.rearrange("(j p) o -> j (p o)", p=P))
        for t in range(1, PACK):
            nc.sync.dma_start(planes[t][:], hid_planes[:, t, :])
        for h, ds in enumerate(halves(D)):
            nc.sync.dma_start(w_raw[h][:], wp.rearrange("(p t) d -> p t d", t=PACK)[:, :, ds])
        nc.sync.dma_start(pages[:], offs2)
        for j in range(D_TILES):
            nc.sync.dma_start(olds[j][:], old[j * P : (j + 1) * P, :])

        ident = keep.tile([P, P], F32, name="ident")
        make_identity(nc, ident[:])
        turned = psum.tile([P, P], F32, name="turned")
        nc.tensor.transpose(turned[:], rows[:], ident[:])
        cols = keep.tile([P, 2 * BIAS_ROW], F32, name="cols")
        nc.vector.tensor_copy(cols[:], turned[:, 0 : 2 * BIAS_ROW])
        fade_banks = [psum.tile([P, BANK], F32, name="fade_bank%d" % h) for h in range(U // BANK)]
        for c in range(U // P):
            h, x = divmod(c * P, BANK)
            nc.tensor.transpose(fade_banks[h][:, x : x + P], cols[:, c : c + 1].to_broadcast([P, P]), ident[:])

        placed = [keep.tile([P, U], F32, name="placed%d" % j) for j in range(D_TILES)]
        for j in range(D_TILES):
            nc.vector.memset(placed[j][:], 0.0)

        sums = reuse.tile([P, PACK, G], F32, name="sums", offset=SUMS_AT, align_bytes=64)
        for t in range(PACK):
            head = keep.tile([P, HEAD], F32, name="head%d" % t)
            tail = keep.tile([P, I - HEAD], F32, name="tail%d" % t)
            nc.vector.tensor_copy(head[:, 0:VECTOR_SHARE], planes[t][:].indirect(slots[:, 0 : VECTOR_SHARE // STRIPE]))
            nc.scalar.activation(
                head[:, VECTOR_SHARE:HEAD], planes[t][:].indirect(slots[:, VECTOR_SHARE // STRIPE : HEAD // STRIPE]), ACT.Copy
            )
            nc.scalar.activation(tail[:], planes[t][:].indirect(slots[:, HEAD // STRIPE : I // STRIPE]), ACT.Copy)
            for piece, lo, hi in ((head, 0, HEAD), (tail, HEAD, I)):
                nc.vector.tensor_reduce(
                    sums[:, t, lo // PAGE : hi // PAGE], piece[:].rearrange("p (g i) -> p g i", i=PAGE), AXIS_X, ALU.add
                )

        def woven(src, dst):
            return src.rearrange("p t (c i) -> p c t i", i=RUN), dst.rearrange("p (c i) t -> p c t i", i=RUN)

        def quantise(codes, scales, values):
            nc.vector.quantize_mx(out=codes.bitcast(FP8X4), scales=scales, in_=values.rearrange("p c t -> p (c t)"))

        w_in = []
        for h in range(2):
            w_in.append(reuse.tile([P, D // 2, PACK], BF16, name="w_in%d" % h, offset=W_IN_AT[h], align_bytes=64))
            src, dst = woven(w_raw[h][:], w_in[h][:])
            nc.scalar.copy(dst, src)

        h_in = []
        for s, gs in enumerate(halves(G)):
            h_in.append(reuse.tile([P, G // 2, PACK], BF16, name="h_in%d" % s, offset=H_IN_AT[s], align_bytes=64))
            src, dst = woven(sums[:, :, gs], h_in[s][:])
            nc.vector.tensor_scalar(dst, src, 1.0 / PAGE, None, ALU.mult)

        w_codes = [
            reuse.tile([P, D // 2], U32, name="w_codes%d" % h, offset=W_CODES_AT[h], align_bytes=64) for h in range(2)
        ]
        w_scales = [keep.tile([P, D // 2], U8, name="w_scales%d" % h, align_bytes=64) for h in range(2)]
        h_codes = keep.tile([P, G], U32, name="h_codes", align_bytes=64)
        h_scales = keep.tile([P, G], U8, name="h_scales", align_bytes=64)
        for s, gs in enumerate(halves(G)):
            quantise(h_codes[:, gs], h_scales[:, gs], h_in[s][:])
            quantise(w_codes[s][:], w_scales[s][:], w_in[s][:])

        z = [psum.tile([P, G], F32, name="z%d" % j) for j in range(D_TILES)]
        for j in range(D_TILES):
            h, m = divmod(j * P, D // 2)
            nc.tensor.matmul_mx(
                out=z[j][:],
                lhsT=w_codes[h][:, m : m + P].bitcast(FP8X4),
                lhsT_scale=w_scales[h][:, m : m + P],
                rhs=h_codes[:].bitcast(FP8X4),
                rhs_scale=h_scales[:],
                start=True,
                stop=True,
            )

        fresh = [keep.tile([P, G], F32, name="fresh%d" % j) for j in range(D_TILES)]

        def squash(j):
            nc.scalar.activation(fresh[j][:], z[j][:], ACT.Tanh, bias=cols[:, BIAS_ROW + j : BIAS_ROW + j + 1])

        squash(0)
        for j in range(D_TILES):
            if j + 1 < D_TILES:
                squash(j + 1)
            nc.scalar.activation(placed[j][:].indirect(pages[:]), fresh[j][:], ACT.Copy)

        last = D_TILES - 1
        faded = [reuse.tile([P, U], F32, name="faded%d" % j, offset=FADED_AT[j], align_bytes=64) for j in range(last)]
        faded.append(faded[0])
        totals = [olds[1], olds[0]] + olds[2:]
        banks = halves(U)

        def fade_old(j, h):
            nc.vector.tensor_tensor(faded[j][:, banks[h]], olds[j][:, banks[h]], fade_banks[h][:], ALU.mult)

        def finish(j, us):
            nc.vector.tensor_tensor(totals[j][:, us], faded[j][:, us], placed[j][:, us], ALU.add)
            nc.sync.dma_start(out[j * P : (j + 1) * P, us], totals[j][:, us])

        whole = slice(0, U)
        for j in range(last):
            for h in range(len(banks)):
                fade_old(j, h)
        for j in range(last - 1):
            finish(j, whole)
        fade_old(last, 0)
        finish(last - 1, whole)
        fade_old(last, 1)
        for us in banks:
            finish(last, us)
